import numpy as np
import ml_dtypes


def mxq(x, axis, fmt="e4m3"):
    dtype, down = {"e4m3": (ml_dtypes.float8_e4m3fn, 7), "e5m2": (ml_dtypes.float8_e5m2, 14)}[fmt]
    v = np.moveaxis(np.asarray(x, np.float32).astype(ml_dtypes.bfloat16).astype(np.float64), axis, -1)
    blocks = v.reshape(v.shape[:-1] + (-1, 32))
    amax = np.abs(blocks).max(-1, keepdims=True)
    byte = np.maximum(np.where(amax > 0, np.frexp(amax)[1] - 1 + 127, 0) - down, 1)
    scale = np.exp2(byte - 127.0)
    codes = (blocks / scale).astype(np.float32).astype(dtype).astype(np.float64)
    return np.moveaxis((codes * scale).reshape(v.shape), -1, axis)


WIDE = False


def mx_kscale(k):
    if not WIDE:
        return np.ones(k)
    levels = np.array([10, -10, 5, -5, 0])
    if k % 512:
        return np.exp2(np.random.permutation(np.resize(levels, k // 32))).repeat(32)
    a = np.empty((k // 512, 16))
    for p in range(k // 512):
        a[p, :8] = np.random.permutation(np.resize(levels, 8))
        for g in range(8):
            far = levels[np.abs(levels - a[p, g]) >= 10]
            a[p, g + 8] = far[np.random.randint(len(far))]
    return np.exp2(a.ravel()).repeat(32)


def f64(x):
    return np.asarray(x).astype(np.float64)


def striped(idx):
    return np.tile(idx.reshape(-1, 16).T, (8, 1)).astype(np.uint16)


def unstriped(offs):
    return offs[:16].T.reshape(-1).astype(np.int64)


def striped8(idx):
    return np.concatenate([x.reshape(-1, 16).T for x in idx]).astype(np.uint16)


def runs(offs, k):
    lists = np.stack([offs[16 * r : 16 * r + 16].T.reshape(-1) for r in range(8)]).astype(np.int64)
    return lists[np.arange(k) % 512 // 64]


def pack_weight(w):
    k, n = w.shape
    w = f64(np.asarray(w, np.float32).astype(ml_dtypes.bfloat16)).reshape(k // 32, 32, n)
    amax = np.abs(w).max(1)
    byte = np.clip(np.where(amax > 0, np.frexp(amax)[1] - 1 + 127 - 7, 1), 1, 254)
    scaled = (w * np.exp2(127.0 - byte)[:, None, :]).reshape(k, n).astype(np.float32)
    words = np.ascontiguousarray(scaled.reshape(k // 512, 128, 4, n).transpose(0, 1, 3, 2)).astype(ml_dtypes.float8_e4m3fn).view(np.uint8)
    return words, np.ascontiguousarray(byte.astype(np.uint8).reshape(k // 512, 16, n))


def unpack_weight(words, scales):
    g, p, n, _ = words.shape
    vals = np.ascontiguousarray(words).view(ml_dtypes.float8_e4m3fn).astype(np.float64) * np.repeat(np.exp2(scales.astype(np.float64) - 127.0), 8, axis=1)[..., None]
    return vals.transpose(0, 1, 3, 2).reshape(g * 512, n)


E2M1 = np.array([0.0, 0.5, 1.0, 1.5, 2.0, 3.0, 4.0, 6.0, -0.0, -0.5, -1.0, -1.5, -2.0, -3.0, -4.0, -6.0])


def pack_fp4(w):
    k, n = w.shape
    w = f64(np.asarray(w, np.float32).astype(ml_dtypes.bfloat16)).reshape(k // 32, 32, n)
    amax = np.abs(w).max(1)
    mant, ex = np.frexp(amax / 6.0)
    byte = np.clip(np.where(amax > 0, np.where(mant > 0.5, ex, ex - 1) + 127, 1), 1, 254)
    scaled = (w * np.exp2(127.0 - byte)[:, None, :]).reshape(k, n).astype(np.float32)
    c = np.ascontiguousarray(scaled.reshape(k // 512, 128, 4, n).transpose(0, 1, 3, 2)).astype(ml_dtypes.float4_e2m1fn).view(np.uint8) & 0xF
    words = (c[..., 0::2] | (c[..., 1::2] << 4)).reshape(k // 512, 128, 2 * n)
    return np.ascontiguousarray(words), np.ascontiguousarray(byte.astype(np.uint8).reshape(k // 512, 16, n))


def unpack_fp4(words, scales):
    g, _, n = scales.shape
    words = np.ascontiguousarray(words).reshape(g, 128, n, 2)
    nib = np.empty((g, 128, n, 4), np.uint8)
    nib[..., 0::2] = words & 0xF
    nib[..., 1::2] = words >> 4
    vals = E2M1[nib] * np.repeat(np.exp2(scales.astype(np.float64) - 127.0), 8, axis=1)[..., None]
    return vals.transpose(0, 1, 3, 2).reshape(g * 512, n)


K, T, S, H, G = 512, 1024, 256, 512, 2048


def setup_inputs():
    n = np.random.standard_normal
    s = mx_kscale(K)[:, None]
    packed_xT = pack_weight(n((K, T)) * s)
    packed_w1 = pack_fp4(n((K, H)) / np.sqrt(K) / s)
    packed_dT = pack_weight(n((K, G)) / s)
    return {
        "x_words": packed_xT[0],
        "x_scales": packed_xT[1],
        "w1_words": packed_w1[0],
        "w1_scales": packed_w1[1],
        "gs": (np.random.uniform(0.5, 1.5, (K, 1)) * s).astype(np.float32),
        "d_words": packed_dT[0],
        "d_scales": packed_dT[1],
        "offs": striped(np.random.permutation(T)[:S]),
        "k1": striped8(np.random.randint(0, G, (8, H))),
        "k2": striped8(np.random.randint(0, G, (8, H))),
        "hz": striped8(np.random.randint(0, T, (8, S))),
        "n1": striped(np.random.permutation(S)),
        "n2": striped(np.random.permutation(S)),
    }


def reference(x_words, x_scales, w1_words, w1_scales, gs, d_words, d_scales, offs, k1, k2, hz, n1, n2):
    d_k1 = unpack_weight(d_words, d_scales)[np.arange(K)[:, None], runs(k1, K)]
    xq = unpack_weight(x_words, x_scales)[:, unstriped(offs)]
    y = unpack_fp4(w1_words, w1_scales).T @ xq
    z = f64(gs) * y
    d_k2 = unpack_weight(d_words, d_scales)[np.arange(K)[:, None], runs(k2, K)]
    x_hz = unpack_weight(x_words, x_scales)[np.arange(K)[:, None], runs(hz, K)]
    h = 0.0625 * ((d_k1.T @ mxq(z, 0, "e4m3") + d_k2.T @ x_hz))
    ds = np.zeros((H, S))
    ds[:, unstriped(n1)] = h
    ds2 = np.zeros((H, S))
    ds2[:, unstriped(n2)] = h
    return np.maximum(ds, ds2)

@@ -1,0 +1,202 @@
+from contextlib import ExitStack
+
+import concourse.mybir as mybir
+
+K, T, S, H, G = 512, 1024, 256, 512, 2048
+FLOPS = 3 * 2 * K * H * S
+
+F32 = mybir.dt.float32
+BF16 = mybir.dt.bfloat16
+I32 = mybir.dt.int32
+U32 = mybir.dt.uint32
+U16 = mybir.dt.uint16
+U8 = mybir.dt.uint8
+FP8X4 = mybir.dt.float8_e4m3fn_x4
+FP4X4 = mybir.dt.float4_e2m1fn_x4
+COPY = mybir.ActivationFunctionType.Copy
+MULT = mybir.AluOpType.mult
+MAX = mybir.AluOpType.max
+
+P = 128
+PACK = 4
+LANES = 16
+HALF = S // 2
+PAIR = 2 * P
+AL = 64
+
+
+def entries(list_tile, first, count):
+    return list_tile[:, first // LANES : (first + count) // LANES]
+
+
+def tile_picked_cmixhisendtwo_none_p_kernel(
+    tc, x_words, x_scales, w1_words, w1_scales, gs, d_words, d_scales, offs, k1, k2, hz, n1, n2, out
+):
+    nc = tc.nc
+    with ExitStack() as ctx:
+        lists = ctx.enter_context(tc.tile_pool(name="lists", bufs=1))
+        keep = ctx.enter_context(tc.tile_pool(name="keep", bufs=1))
+        psum = ctx.enter_context(tc.psum_pool(name="psum", bufs=1))
+
+        d_sc = keep.tile([P, G], U8, align_bytes=AL, name="d_sc")
+        x_sc = keep.tile([P, T], U8, align_bytes=AL, name="x_sc")
+        w_sc = keep.tile([P, H], U8, align_bytes=AL, name="w_sc")
+        plane_a = keep.tile([P, 2 * PAIR + 2 * HALF], U8, align_bytes=AL, name="plane_a")
+        plane_k = keep.tile([P, 2 * PAIR], U8, align_bytes=AL, name="plane_k")
+        plane_x = keep.tile([P, 2 * HALF], U8, align_bytes=AL, name="plane_x")
+        for t in (d_sc, x_sc, w_sc, plane_a, plane_k, plane_x):
+            nc.vector.memset(t[:].bitcast(I32), 0)
+
+        def load_list(src, name):
+            t = lists.tile(list(src.shape), U16, name=name)
+            nc.sync.dma_start(t[:], src)
+            return t
+
+        x_w = keep.tile([P, T], U32, align_bytes=AL, name="x_w")
+        d_w = keep.tile([P, G], U32, align_bytes=AL, name="d_w")
+        w_w = keep.tile([P, 2 * H], U8, align_bytes=AL, name="w_w")
+        nc.scalar.dma_start(x_w[:].bitcast(I32), x_words[0].rearrange("p n t -> p (n t)").bitcast(I32))
+        nc.scalar.dma_start(w_w[:].bitcast(I32), w1_words[0].bitcast(I32))
+        nc.scalar.dma_start(d_w[:].bitcast(I32), d_words[0].rearrange("p n t -> p (n t)").bitcast(I32))
+
+        k1_l = load_list(k1, "k1_l")
+        k2_l = load_list(k2, "k2_l")
+        nc.sync.dma_start(d_sc[0:P:8, :].bitcast(I32), d_scales[0].bitcast(I32))
+        nc.sync.dma_start(x_sc[0:P:8, :].bitcast(I32), x_scales[0].bitcast(I32))
+        hz_l = load_list(hz, "hz_l")
+        offs_l = load_list(offs, "offs_l")
+        for q in range(4):
+            queue = nc.sync if q < 3 else nc.gpsimd
+            queue.dma_start(w_sc[32 * q : 32 * q + 4, :].bitcast(I32), w1_scales[0, 4 * q : 4 * q + 4, :].bitcast(I32))
+        n1_l = load_list(n1, "n1_l")
+        n2_l = load_list(n2, "n2_l")
+        gain = keep.tile([P, PACK], F32, name="gain")
+        nc.gpsimd.dma_start(gain[:], gs.rearrange("(p t) o -> p (t o)", t=PACK))
+
+        w_dw = keep.tile([P, 2 * H], U8, align_bytes=AL, name="w_dw")
+        w_ds = keep.tile([P, H], U8, align_bytes=AL, name="w_ds")
+        nc.scalar.copy(
+            w_dw[:].bitcast(U16).rearrange("p (t m) -> p t m", t=PACK),
+            w_w[:].bitcast(U16).rearrange("p (m t) -> p t m", t=PACK),
+        )
+        nc.gpsimd.tensor_copy(
+            w_ds[:].rearrange("p (t m) -> p t m", t=PACK),
+            w_sc[:].rearrange("p (m t) -> p t m", t=PACK),
+        )
+
+        def gather(dst, window, offsets):
+            nc.vector.tensor_copy(dst, window[:].indirect(offsets))
+
+        def gather_bytes(jobs, tag, plane, queue):
+            width = sum(n for (w, l, f, n) in jobs)
+            picked = keep.tile([P, width], U8, align_bytes=AL, tag=tag, name="picked")
+            at = 0
+            for window, list_tile, first, n in jobs:
+                gather(picked[:, at : at + n], window, entries(list_tile, first, n))
+                at = at + n
+            for r in range(4):
+                queue.dma_start(plane[r:P:32, :].bitcast(I32), picked[8 * r : P : 32, :].bitcast(I32))
+
+        def gather_words(window, list_tile, first, n, tag):
+            words = keep.tile([P, n], U32, align_bytes=AL, tag=tag, name="words")
+            gather(words[:], window, entries(list_tile, first, n))
+            return words
+
+        def project(xo_w, xo_s, tag):
+            y = psum.tile([P, PACK, HALF], F32, tag="y_" + tag, name="y")
+            for t in range(PACK):
+                nc.tensor.matmul_mx(
+                    y[:, t, :],
+                    lhsT=w_dw[:, 2 * P * t : 2 * P * (t + 1)].bitcast(FP4X4),
+                    lhsT_scale=w_ds[:, P * t : P * (t + 1)],
+                    rhs=xo_w[:].bitcast(FP8X4),
+                    rhs_scale=xo_s,
+                    start=True,
+                    stop=True,
+                )
+            z = keep.tile([P, HALF, PACK], BF16, align_bytes=AL, tag="z_" + tag, name="z")
+            nc.vector.tensor_tensor(
+                z[:], y[:].rearrange("p t j -> p j t"), gain[:].unsqueeze(1).to_broadcast([P, HALF, PACK]), MULT
+            )
+            z_w = keep.tile([P, HALF], U32, align_bytes=AL, tag="zw_" + tag, name="z_w")
+            z_s = keep.tile([P, HALF], U8, align_bytes=AL, tag="zs_" + tag, name="z_s")
+            nc.vector.quantize_mx(z_w[:].bitcast(FP8X4), z_s[:], z[:].rearrange("p j t -> p (j t)"))
+            return z_w, z_s
+
+        def hashed_pass(acc, k2_w, k2_s, m, hz_w, hz_s):
+            nc.tensor.matmul_mx(
+                acc, lhsT=k2_w[:, P * m : P * (m + 1)].bitcast(FP8X4), lhsT_scale=k2_s[:, P * m : P * (m + 1)],
+                rhs=hz_w[:].bitcast(FP8X4), rhs_scale=hz_s, start=True, stop=False,
+            )
+
+        def projected_pass(acc, k1_w, k1_s, m, z_w, z_s):
+            nc.tensor.matmul_mx(
+                acc, lhsT=k1_w[:, P * m : P * (m + 1)].bitcast(FP8X4), lhsT_scale=k1_s[:, P * m : P * (m + 1)],
+                rhs=z_w[:].bitcast(FP8X4), rhs_scale=z_s[:], start=False, stop=True,
+            )
+
+        widths = [S, S, 2 * S, 2 * S]
+        ds1 = [keep.tile([P, widths[m]], F32, name="ds1_%d" % m) for m in range(4)]
+        ds2 = [keep.tile([P, widths[m]], F32, name="ds2_%d" % m) for m in range(4)]
+
+        def send(h, m, first, n):
+            nc.scalar.activation(ds1[m][:].indirect(entries(n1_l, first, n)), h, COPY)
+            nc.scalar.activation(ds2[m][:].indirect(entries(n2_l, first, n)), h, COPY)
+
+        def finish(m):
+            larger = keep.tile([P, S], F32, name="larger_%d" % m)
+            nc.vector.tensor_tensor(larger[:], ds1[m][:, 0:S], ds2[m][:, 0:S], MAX)
+            nc.sync.dma_start(out[P * m : P * (m + 1), :], larger[:])
+
+        gather_bytes(
+            [(d_sc, k1_l, 0, PAIR), (d_sc, k2_l, 0, PAIR), (x_sc, hz_l, 0, HALF), (x_sc, offs_l, 0, HALF)],
+            "picked_a", plane_a, nc.scalar,
+        )
+        k1a_s, k2a_s = plane_a[:, 0:PAIR], plane_a[:, PAIR : 2 * PAIR]
+        hza_s, xoa_s = plane_a[:, 2 * PAIR : 2 * PAIR + HALF], plane_a[:, 2 * PAIR + HALF :]
+        xoa_w = gather_words(x_w, offs_l, 0, HALF, "xo_w")
+        hza_w = gather_words(x_w, hz_l, 0, HALF, "hza_w")
+        gather_bytes([(x_sc, offs_l, HALF, HALF), (x_sc, hz_l, HALF, HALF)], "picked_x", plane_x, nc.sync)
+        xob_s, hzb_s = plane_x[:, 0:HALF], plane_x[:, HALF:]
+        k2a_w = gather_words(d_w, k2_l, 0, PAIR, "k2_w")
+        k1a_w = gather_words(d_w, k1_l, 0, PAIR, "k1_w")
+        za_w, za_s = project(xoa_w, xoa_s, "a")
+        first = [psum.tile([P, HALF], F32, name="first_%d" % m) for m in range(2)]
+        for m in range(2):
+            hashed_pass(first[m][:], k2a_w, k2a_s, m, hza_w, hza_s)
+        for m in range(2):
+            projected_pass(first[m][:], k1a_w, k1a_s, m, za_w, za_s)
+        h0 = keep.tile([P, HALF], F32, align_bytes=AL, tag="h0", name="h0")
+        nc.scalar.activation(h0[:], first[0][:], COPY, scale=0.0625)
+        send(h0[:], 0, 0, HALF)
+        h1 = keep.tile([P, HALF], F32, align_bytes=AL, tag="h1", name="h1")
+        nc.vector.tensor_scalar(h1[:], first[1][:], 0.0625, None, MULT)
+        send(h1[:], 1, 0, HALF)
+
+        xob_w = gather_words(x_w, offs_l, HALF, HALF, "xo_w")
+        hzb_w = gather_words(x_w, hz_l, HALF, HALF, "z_a")
+        zb_w, zb_s = project(xob_w, xob_s, "b")
+        second = psum.tile([P, 2, HALF], F32, name="second")
+        for m in range(2):
+            hashed_pass(second[:, m, :], k2a_w, k2a_s, m, hzb_w, hzb_s)
+            projected_pass(second[:, m, :], k1a_w, k1a_s, m, zb_w, zb_s)
+        h01 = keep.tile([P, 2, HALF], F32, name="h01")
+        nc.vector.tensor_scalar(h01[:], second[:], 0.0625, None, MULT)
+        for m in range(2):
+            send(h01[:, m, :], m, HALF, HALF)
+
+        gather_bytes([(d_sc, k1_l, PAIR, PAIR), (d_sc, k2_l, PAIR, PAIR)], "h0", plane_k, nc.sync)
+        k1b_s, k2b_s = plane_k[:, 0:PAIR], plane_k[:, PAIR:]
+        k2b_w = gather_words(d_w, k2_l, PAIR, PAIR, "k2_w")
+        k1b_w = gather_words(d_w, k1_l, PAIR, PAIR, "k1_w")
+        halves = [(hza_w, hza_s, za_w, za_s), (hzb_w, hzb_s, zb_w, zb_s)]
+        for m in range(2):
+            acc = psum.tile([P, 2, HALF], F32, name="acc_%d" % m)
+            for c, (hz_w, hz_s, z_w, z_s) in enumerate(halves):
+                hashed_pass(acc[:, c, :], k2b_w, k2b_s, m, hz_w, hz_s)
+                projected_pass(acc[:, c, :], k1b_w, k1b_s, m, z_w, z_s)
+            h = keep.tile([P, S], F32, name="h_%d" % m)
+            nc.vector.tensor_scalar(h[:], acc[:].rearrange("p c j -> p (c j)"), 0.0625, None, MULT)
+            send(h[:], 2 + m, 0, S)
+        for m in range(4):
+            finish(m)

@@ -21,6 +21,7 @@ P = 128
 PACK = 4
 LANES = 16
 HALF = S // 2
+QUARTER = S // 4
 PAIR = 2 * P
 AL = 64
 
@@ -41,11 +42,12 @@ def tile_picked_cmixhisendtwo_none_p_kernel(
         d_sc = keep.tile([P, G], U8, align_bytes=AL, name="d_sc")
         x_sc = keep.tile([P, T], U8, align_bytes=AL, name="x_sc")
         w_sc = keep.tile([P, H], U8, align_bytes=AL, name="w_sc")
-        plane_a = keep.tile([P, 2 * PAIR + 2 * HALF], U8, align_bytes=AL, name="plane_a")
+        plane_a = keep.tile([P, 2 * PAIR + S + HALF], U8, align_bytes=AL, name="plane_a")
         plane_k = keep.tile([P, 2 * PAIR], U8, align_bytes=AL, name="plane_k")
-        plane_x = keep.tile([P, 2 * HALF], U8, align_bytes=AL, name="plane_x")
-        for t in (d_sc, x_sc, w_sc, plane_a, plane_k, plane_x):
+        plane_x = keep.tile([P, HALF], U8, align_bytes=AL, name="plane_x")
+        for t in (x_sc, d_sc, plane_a, plane_k, plane_x):
             nc.vector.memset(t[:].bitcast(I32), 0)
+        nc.gpsimd.memset(w_sc[:].bitcast(I32), 0)
 
         def load_list(src, name):
             t = lists.tile(list(src.shape), U16, name=name)
@@ -55,23 +57,20 @@ def tile_picked_cmixhisendtwo_none_p_kernel(
         x_w = keep.tile([P, T], U32, align_bytes=AL, name="x_w")
         d_w = keep.tile([P, G], U32, align_bytes=AL, name="d_w")
         w_w = keep.tile([P, 2 * H], U8, align_bytes=AL, name="w_w")
-        nc.scalar.dma_start(x_w[:].bitcast(I32), x_words[0].rearrange("p n t -> p (n t)").bitcast(I32))
         nc.scalar.dma_start(w_w[:].bitcast(I32), w1_words[0].bitcast(I32))
+        nc.scalar.dma_start(x_sc[0:P:8, :].bitcast(I32), x_scales[0].bitcast(I32))
+        nc.scalar.dma_start(d_sc[0:P:8, :].bitcast(I32), d_scales[0].bitcast(I32))
         nc.scalar.dma_start(d_w[:].bitcast(I32), d_words[0].rearrange("p n t -> p (n t)").bitcast(I32))
 
+        hz_l = load_list(hz, "hz_l")
         k1_l = load_list(k1, "k1_l")
         k2_l = load_list(k2, "k2_l")
-        nc.sync.dma_start(d_sc[0:P:8, :].bitcast(I32), d_scales[0].bitcast(I32))
-        nc.sync.dma_start(x_sc[0:P:8, :].bitcast(I32), x_scales[0].bitcast(I32))
-        hz_l = load_list(hz, "hz_l")
         offs_l = load_list(offs, "offs_l")
         for q in range(4):
-            queue = nc.sync if q < 3 else nc.gpsimd
+            queue = nc.sync if q < 2 else nc.gpsimd
             queue.dma_start(w_sc[32 * q : 32 * q + 4, :].bitcast(I32), w1_scales[0, 4 * q : 4 * q + 4, :].bitcast(I32))
-        n1_l = load_list(n1, "n1_l")
-        n2_l = load_list(n2, "n2_l")
+        nc.sync.dma_start(x_w[:].bitcast(I32), x_words[0].rearrange("p n t -> p (n t)").bitcast(I32))
         gain = keep.tile([P, PACK], F32, name="gain")
-        nc.gpsimd.dma_start(gain[:], gs.rearrange("(p t) o -> p (t o)", t=PACK))
 
         w_dw = keep.tile([P, 2 * H], U8, align_bytes=AL, name="w_dw")
         w_ds = keep.tile([P, H], U8, align_bytes=AL, name="w_ds")
@@ -87,7 +86,7 @@ def tile_picked_cmixhisendtwo_none_p_kernel(
         def gather(dst, window, offsets):
             nc.vector.tensor_copy(dst, window[:].indirect(offsets))
 
-        def gather_bytes(jobs, tag, plane, queue):
+        def gather_bytes(jobs, tag, plane, queues):
             width = sum(n for (w, l, f, n) in jobs)
             picked = keep.tile([P, width], U8, align_bytes=AL, tag=tag, name="picked")
             at = 0
@@ -95,15 +94,15 @@ def tile_picked_cmixhisendtwo_none_p_kernel(
                 gather(picked[:, at : at + n], window, entries(list_tile, first, n))
                 at = at + n
             for r in range(4):
-                queue.dma_start(plane[r:P:32, :].bitcast(I32), picked[8 * r : P : 32, :].bitcast(I32))
+                queues[r % len(queues)].dma_start(plane[r:P:32, :].bitcast(I32), picked[8 * r : P : 32, :].bitcast(I32))
 
         def gather_words(window, list_tile, first, n, tag):
             words = keep.tile([P, n], U32, align_bytes=AL, tag=tag, name="words")
             gather(words[:], window, entries(list_tile, first, n))
             return words
 
-        def project(xo_w, xo_s, tag):
-            y = psum.tile([P, PACK, HALF], F32, tag="y_" + tag, name="y")
+        def project(xo_w, xo_s, tag, bank):
+            y = psum.tile([P, PACK, HALF], F32, tag=bank, name="y")
             for t in range(PACK):
                 nc.tensor.matmul_mx(
                     y[:, t, :],
@@ -114,13 +113,17 @@ def tile_picked_cmixhisendtwo_none_p_kernel(
                     start=True,
                     stop=True,
                 )
-            z = keep.tile([P, HALF, PACK], BF16, align_bytes=AL, tag="z_" + tag, name="z")
-            nc.vector.tensor_tensor(
-                z[:], y[:].rearrange("p t j -> p j t"), gain[:].unsqueeze(1).to_broadcast([P, HALF, PACK]), MULT
-            )
             z_w = keep.tile([P, HALF], U32, align_bytes=AL, tag="zw_" + tag, name="z_w")
             z_s = keep.tile([P, HALF], U8, align_bytes=AL, tag="zs_" + tag, name="z_s")
-            nc.vector.quantize_mx(z_w[:].bitcast(FP8X4), z_s[:], z[:].rearrange("p j t -> p (j t)"))
+            parts = [slice(0, QUARTER), slice(QUARTER, HALF)]
+            z = [keep.tile([P, QUARTER, PACK], BF16, align_bytes=AL, tag="z%d_%s" % (c, tag), name="z") for c in range(2)]
+            for c in range(2):
+                nc.vector.tensor_tensor(
+                    z[c][:], y[:, :, parts[c]].rearrange("p t j -> p j t"),
+                    gain[:].unsqueeze(1).to_broadcast([P, QUARTER, PACK]), MULT,
+                )
+            for c in range(2):
+                nc.vector.quantize_mx(z_w[:, parts[c]].bitcast(FP8X4), z_s[:, parts[c]], z[c][:].rearrange("p j t -> p (j t)"))
             return z_w, z_s
 
         def hashed_pass(acc, k2_w, k2_s, m, hz_w, hz_s):
@@ -143,25 +146,30 @@ def tile_picked_cmixhisendtwo_none_p_kernel(
             nc.scalar.activation(ds1[m][:].indirect(entries(n1_l, first, n)), h, COPY)
             nc.scalar.activation(ds2[m][:].indirect(entries(n2_l, first, n)), h, COPY)
 
-        def finish(m):
-            larger = keep.tile([P, S], F32, name="larger_%d" % m)
-            nc.vector.tensor_tensor(larger[:], ds1[m][:, 0:S], ds2[m][:, 0:S], MAX)
-            nc.sync.dma_start(out[P * m : P * (m + 1), :], larger[:])
+        def finish(m, tag, cols, queue):
+            larger = keep.tile([P, cols.stop - cols.start], F32, align_bytes=AL, tag=tag, name="larger")
+            nc.vector.tensor_tensor(larger[:], ds1[m][:, cols], ds2[m][:, cols], MAX)
+            queue.dma_start(out[P * m : P * (m + 1), cols], larger[:])
 
         gather_bytes(
-            [(d_sc, k1_l, 0, PAIR), (d_sc, k2_l, 0, PAIR), (x_sc, hz_l, 0, HALF), (x_sc, offs_l, 0, HALF)],
-            "picked_a", plane_a, nc.scalar,
+            [(x_sc, hz_l, 0, S), (d_sc, k1_l, 0, PAIR), (d_sc, k2_l, 0, PAIR), (x_sc, offs_l, 0, HALF)],
+            "picked_a", plane_a, [nc.scalar, nc.sync],
         )
-        k1a_s, k2a_s = plane_a[:, 0:PAIR], plane_a[:, PAIR : 2 * PAIR]
-        hza_s, xoa_s = plane_a[:, 2 * PAIR : 2 * PAIR + HALF], plane_a[:, 2 * PAIR + HALF :]
-        xoa_w = gather_words(x_w, offs_l, 0, HALF, "xo_w")
-        hza_w = gather_words(x_w, hz_l, 0, HALF, "hza_w")
-        gather_bytes([(x_sc, offs_l, HALF, HALF), (x_sc, hz_l, HALF, HALF)], "picked_x", plane_x, nc.sync)
-        xob_s, hzb_s = plane_x[:, 0:HALF], plane_x[:, HALF:]
+        hza_s, hzb_s = plane_a[:, 0:HALF], plane_a[:, HALF:S]
+        k1a_s, k2a_s = plane_a[:, S : S + PAIR], plane_a[:, S + PAIR : S + 2 * PAIR]
+        xoa_s = plane_a[:, S + 2 * PAIR :]
+        nc.sync.dma_start(gain[:], gs.rearrange("(p t) o -> p (t o)", t=PACK))
+        n1_l = load_list(n1, "n1_l")
+        n2_l = load_list(n2, "n2_l")
+        gather_bytes([(x_sc, offs_l, HALF, HALF)], "picked_x", plane_x, [nc.sync])
+        xob_s = plane_x[:]
         k2a_w = gather_words(d_w, k2_l, 0, PAIR, "k2_w")
         k1a_w = gather_words(d_w, k1_l, 0, PAIR, "k1_w")
-        za_w, za_s = project(xoa_w, xoa_s, "a")
-        first = [psum.tile([P, HALF], F32, name="first_%d" % m) for m in range(2)]
+        xoa_w = gather_words(x_w, offs_l, 0, HALF, "xo_w")
+        hza_w = gather_words(x_w, hz_l, 0, HALF, "hza_w")
+        hzb_w = gather_words(x_w, hz_l, HALF, HALF, "hzb_w")
+        za_w, za_s = project(xoa_w, xoa_s, "a", "y_a")
+        first = [psum.tile([P, HALF], F32, tag="first_%d" % m, name="first") for m in range(2)]
         for m in range(2):
             hashed_pass(first[m][:], k2a_w, k2a_s, m, hza_w, hza_s)
         for m in range(2):
@@ -173,9 +181,9 @@ def tile_picked_cmixhisendtwo_none_p_kernel(
         nc.vector.tensor_scalar(h1[:], first[1][:], 0.0625, None, MULT)
         send(h1[:], 1, 0, HALF)
 
-        xob_w = gather_words(x_w, offs_l, HALF, HALF, "xo_w")
-        hzb_w = gather_words(x_w, hz_l, HALF, HALF, "z_a")
-        zb_w, zb_s = project(xob_w, xob_s, "b")
+        gather_bytes([(d_sc, k1_l, PAIR, PAIR), (d_sc, k2_l, PAIR, PAIR)], "z0_a", plane_k, [nc.sync])
+        xob_w = gather_words(x_w, offs_l, HALF, HALF, "z1_a")
+        zb_w, zb_s = project(xob_w, xob_s, "b", "first_0")
         second = psum.tile([P, 2, HALF], F32, name="second")
         for m in range(2):
             hashed_pass(second[:, m, :], k2a_w, k2a_s, m, hzb_w, hzb_s)
@@ -185,7 +193,6 @@ def tile_picked_cmixhisendtwo_none_p_kernel(
         for m in range(2):
             send(h01[:, m, :], m, HALF, HALF)
 
-        gather_bytes([(d_sc, k1_l, PAIR, PAIR), (d_sc, k2_l, PAIR, PAIR)], "h0", plane_k, nc.sync)
         k1b_s, k2b_s = plane_k[:, 0:PAIR], plane_k[:, PAIR:]
         k2b_w = gather_words(d_w, k2_l, PAIR, PAIR, "k2_w")
         k1b_w = gather_words(d_w, k1_l, PAIR, PAIR, "k1_w")
@@ -198,5 +205,7 @@ def tile_picked_cmixhisendtwo_none_p_kernel(
             h = keep.tile([P, S], F32, name="h_%d" % m)
             nc.vector.tensor_scalar(h[:], acc[:].rearrange("p c j -> p (c j)"), 0.0625, None, MULT)
             send(h[:], 2 + m, 0, S)
-        for m in range(4):
-            finish(m)
+        for m, tag in enumerate(("k1_w", "k2_w", "larger_2")):
+            finish(m, tag, slice(0, S), nc.sync)
+        finish(3, "larger_3a", slice(0, HALF), nc.sync)
+        finish(3, "larger_3b", slice(HALF, S), nc.scalar)

@@ -24,6 +24,7 @@ HALF = S // 2
 QUARTER = S // 4
 PAIR = 2 * P
 AL = 64
+CLEAR_SPLIT = G // 4
 
 
 def entries(list_tile, first, count):
@@ -42,12 +43,14 @@ def tile_picked_cmixhisendtwo_none_p_kernel(
         d_sc = keep.tile([P, G], U8, align_bytes=AL, name="d_sc")
         x_sc = keep.tile([P, T], U8, align_bytes=AL, name="x_sc")
         w_sc = keep.tile([P, H], U8, align_bytes=AL, name="w_sc")
-        plane_a = keep.tile([P, 2 * PAIR + S + HALF], U8, align_bytes=AL, name="plane_a")
+        plane_a = keep.tile([P, 2 * PAIR + S], U8, align_bytes=AL, name="plane_a")
         plane_k = keep.tile([P, 2 * PAIR], U8, align_bytes=AL, name="plane_k")
-        plane_x = keep.tile([P, HALF], U8, align_bytes=AL, name="plane_x")
-        for t in (x_sc, d_sc, plane_a, plane_k, plane_x):
+        plane_x = keep.tile([P, S], U8, align_bytes=AL, name="plane_x")
+        nc.vector.memset(x_sc[:].bitcast(I32), 0)
+        nc.vector.memset(d_sc[:, 0:CLEAR_SPLIT].bitcast(I32), 0)
+        nc.gpsimd.memset(d_sc[:, CLEAR_SPLIT:].bitcast(I32), 0)
+        for t in (w_sc, plane_x, plane_a, plane_k):
             nc.vector.memset(t[:].bitcast(I32), 0)
-        nc.gpsimd.memset(w_sc[:].bitcast(I32), 0)
 
         def load_list(src, name):
             t = lists.tile(list(src.shape), U16, name=name)
@@ -60,17 +63,18 @@ def tile_picked_cmixhisendtwo_none_p_kernel(
         nc.scalar.dma_start(w_w[:].bitcast(I32), w1_words[0].bitcast(I32))
         nc.scalar.dma_start(x_sc[0:P:8, :].bitcast(I32), x_scales[0].bitcast(I32))
         nc.scalar.dma_start(d_sc[0:P:8, :].bitcast(I32), d_scales[0].bitcast(I32))
-        nc.scalar.dma_start(d_w[:].bitcast(I32), d_words[0].rearrange("p n t -> p (n t)").bitcast(I32))
+        nc.scalar.dma_start(x_w[:].bitcast(I32), x_words[0].rearrange("p n t -> p (n t)").bitcast(I32))
 
-        hz_l = load_list(hz, "hz_l")
-        k1_l = load_list(k1, "k1_l")
-        k2_l = load_list(k2, "k2_l")
         offs_l = load_list(offs, "offs_l")
+        k1_l = load_list(k1, "k1_l")
+        hz_l = load_list(hz, "hz_l")
+        k2_l = load_list(k2, "k2_l")
         for q in range(4):
-            queue = nc.sync if q < 2 else nc.gpsimd
+            queue = nc.sync if q < 3 else nc.scalar
             queue.dma_start(w_sc[32 * q : 32 * q + 4, :].bitcast(I32), w1_scales[0, 4 * q : 4 * q + 4, :].bitcast(I32))
-        nc.sync.dma_start(x_w[:].bitcast(I32), x_words[0].rearrange("p n t -> p (n t)").bitcast(I32))
+        nc.sync.dma_start(d_w[:].bitcast(I32), d_words[0].rearrange("p n t -> p (n t)").bitcast(I32))
         gain = keep.tile([P, PACK], F32, name="gain")
+        nc.gpsimd.dma_start(gain[:], gs.rearrange("(p t) o -> p (t o)", t=PACK))
 
         w_dw = keep.tile([P, 2 * H], U8, align_bytes=AL, name="w_dw")
         w_ds = keep.tile([P, H], U8, align_bytes=AL, name="w_ds")
@@ -86,14 +90,14 @@ def tile_picked_cmixhisendtwo_none_p_kernel(
         def gather(dst, window, offsets):
             nc.vector.tensor_copy(dst, window[:].indirect(offsets))
 
-        def gather_bytes(jobs, tag, plane, queues):
-            width = sum(n for (w, l, f, n) in jobs)
-            picked = keep.tile([P, width], U8, align_bytes=AL, tag=tag, name="picked")
+        def gather_bytes(jobs, picked):
             at = 0
             for window, list_tile, first, n in jobs:
                 gather(picked[:, at : at + n], window, entries(list_tile, first, n))
                 at = at + n
-            for r in range(4):
+
+        def place_rows(plane, picked, rows, queues):
+            for r in rows:
                 queues[r % len(queues)].dma_start(plane[r:P:32, :].bitcast(I32), picked[8 * r : P : 32, :].bitcast(I32))
 
         def gather_words(window, list_tile, first, n, tag):
@@ -101,7 +105,7 @@ def tile_picked_cmixhisendtwo_none_p_kernel(
             gather(words[:], window, entries(list_tile, first, n))
             return words
 
-        def project(xo_w, xo_s, tag, bank):
+        def project(xo_w, xo_s, z, tag, bank):
             y = psum.tile([P, PACK, HALF], F32, tag=bank, name="y")
             for t in range(PACK):
                 nc.tensor.matmul_mx(
@@ -116,14 +120,13 @@ def tile_picked_cmixhisendtwo_none_p_kernel(
             z_w = keep.tile([P, HALF], U32, align_bytes=AL, tag="zw_" + tag, name="z_w")
             z_s = keep.tile([P, HALF], U8, align_bytes=AL, tag="zs_" + tag, name="z_s")
             parts = [slice(0, QUARTER), slice(QUARTER, HALF)]
-            z = [keep.tile([P, QUARTER, PACK], BF16, align_bytes=AL, tag="z%d_%s" % (c, tag), name="z") for c in range(2)]
             for c in range(2):
                 nc.vector.tensor_tensor(
-                    z[c][:], y[:, :, parts[c]].rearrange("p t j -> p j t"),
+                    z[:, parts[c], :], y[:, :, parts[c]].rearrange("p t j -> p j t"),
                     gain[:].unsqueeze(1).to_broadcast([P, QUARTER, PACK]), MULT,
                 )
             for c in range(2):
-                nc.vector.quantize_mx(z_w[:, parts[c]].bitcast(FP8X4), z_s[:, parts[c]], z[c][:].rearrange("p j t -> p (j t)"))
+                nc.vector.quantize_mx(z_w[:, parts[c]].bitcast(FP8X4), z_s[:, parts[c]], z[:, parts[c], :].rearrange("p j t -> p (j t)"))
             return z_w, z_s
 
         def hashed_pass(acc, k2_w, k2_s, m, hz_w, hz_s):
@@ -146,29 +149,30 @@ def tile_picked_cmixhisendtwo_none_p_kernel(
             nc.scalar.activation(ds1[m][:].indirect(entries(n1_l, first, n)), h, COPY)
             nc.scalar.activation(ds2[m][:].indirect(entries(n2_l, first, n)), h, COPY)
 
-        def finish(m, tag, cols, queue):
-            larger = keep.tile([P, cols.stop - cols.start], F32, align_bytes=AL, tag=tag, name="larger")
-            nc.vector.tensor_tensor(larger[:], ds1[m][:, cols], ds2[m][:, cols], MAX)
-            queue.dma_start(out[P * m : P * (m + 1), cols], larger[:])
+        def finish(m, tag):
+            larger = keep.tile([P, S], F32, align_bytes=AL, tag=tag, name="larger")
+            nc.vector.tensor_tensor(larger[:], ds1[m][:, 0:S], ds2[m][:, 0:S], MAX)
+            nc.sync.dma_start(out[P * m : P * (m + 1), :], larger[:])
 
-        gather_bytes(
-            [(x_sc, hz_l, 0, S), (d_sc, k1_l, 0, PAIR), (d_sc, k2_l, 0, PAIR), (x_sc, offs_l, 0, HALF)],
-            "picked_a", plane_a, [nc.scalar, nc.sync],
-        )
-        hza_s, hzb_s = plane_a[:, 0:HALF], plane_a[:, HALF:S]
-        k1a_s, k2a_s = plane_a[:, S : S + PAIR], plane_a[:, S + PAIR : S + 2 * PAIR]
-        xoa_s = plane_a[:, S + 2 * PAIR :]
-        nc.sync.dma_start(gain[:], gs.rearrange("(p t) o -> p (t o)", t=PACK))
+        picked_x = keep.tile([P, S], U8, align_bytes=AL, name="picked_x")
+        gather_bytes([(x_sc, offs_l, 0, S)], picked_x)
+        place_rows(plane_x, picked_x, range(4), [nc.sync])
+        xoa_s, xob_s = plane_x[:, 0:HALF], plane_x[:, HALF:]
+        picked_a = keep.tile([P, 2 * PAIR + S], U8, align_bytes=AL, name="picked_a")
+        gather_bytes([(d_sc, k1_l, 0, PAIR), (d_sc, k2_l, 0, PAIR), (x_sc, hz_l, 0, S)], picked_a)
+        place_rows(plane_a, picked_a, range(4), [nc.sync])
+        k1a_s, k2a_s = plane_a[:, 0:PAIR], plane_a[:, PAIR : 2 * PAIR]
+        hza_s, hzb_s = plane_a[:, 2 * PAIR : 2 * PAIR + HALF], plane_a[:, 2 * PAIR + HALF :]
         n1_l = load_list(n1, "n1_l")
         n2_l = load_list(n2, "n2_l")
-        gather_bytes([(x_sc, offs_l, HALF, HALF)], "picked_x", plane_x, [nc.sync])
-        xob_s = plane_x[:]
-        k2a_w = gather_words(d_w, k2_l, 0, PAIR, "k2_w")
-        k1a_w = gather_words(d_w, k1_l, 0, PAIR, "k1_w")
         xoa_w = gather_words(x_w, offs_l, 0, HALF, "xo_w")
         hza_w = gather_words(x_w, hz_l, 0, HALF, "hza_w")
         hzb_w = gather_words(x_w, hz_l, HALF, HALF, "hzb_w")
-        za_w, za_s = project(xoa_w, xoa_s, "a", "y_a")
+        xob_w = gather_words(x_w, offs_l, HALF, HALF, "xob_w")
+        k2a_w = gather_words(d_w, k2_l, 0, PAIR, "k2_w")
+        k1a_w = gather_words(d_w, k1_l, 0, PAIR, "k1_w")
+        z_a = keep.tile([P, HALF, PACK], BF16, align_bytes=AL, tag="z_a", name="z_a")
+        za_w, za_s = project(xoa_w, xoa_s, z_a, "a", "y_a")
         first = [psum.tile([P, HALF], F32, tag="first_%d" % m, name="first") for m in range(2)]
         for m in range(2):
             hashed_pass(first[m][:], k2a_w, k2a_s, m, hza_w, hza_s)
@@ -181,17 +185,20 @@ def tile_picked_cmixhisendtwo_none_p_kernel(
         nc.vector.tensor_scalar(h1[:], first[1][:], 0.0625, None, MULT)
         send(h1[:], 1, 0, HALF)
 
-        gather_bytes([(d_sc, k1_l, PAIR, PAIR), (d_sc, k2_l, PAIR, PAIR)], "z0_a", plane_k, [nc.sync])
-        xob_w = gather_words(x_w, offs_l, HALF, HALF, "z1_a")
-        zb_w, zb_s = project(xob_w, xob_s, "b", "first_0")
-        second = psum.tile([P, 2, HALF], F32, name="second")
+        picked_k = keep.tile([P, 2 * PAIR], U8, align_bytes=AL, tag="z_a", name="picked_k")
+        gather_bytes([(d_sc, k1_l, PAIR, PAIR), (d_sc, k2_l, PAIR, PAIR)], picked_k)
+        place_rows(plane_k, picked_k, range(4), [nc.sync])
+        z_b = keep.tile([P, HALF, PACK], BF16, align_bytes=AL, name="z_b")
+        zb_w, zb_s = project(xob_w, xob_s, z_b, "b", "first_0")
+        second = [psum.tile([P, HALF], F32, name="second_%d" % m) for m in range(2)]
         for m in range(2):
-            hashed_pass(second[:, m, :], k2a_w, k2a_s, m, hzb_w, hzb_s)
-            projected_pass(second[:, m, :], k1a_w, k1a_s, m, zb_w, zb_s)
-        h01 = keep.tile([P, 2, HALF], F32, name="h01")
-        nc.vector.tensor_scalar(h01[:], second[:], 0.0625, None, MULT)
+            hashed_pass(second[m][:], k2a_w, k2a_s, m, hzb_w, hzb_s)
         for m in range(2):
-            send(h01[:, m, :], m, HALF, HALF)
+            projected_pass(second[m][:], k1a_w, k1a_s, m, zb_w, zb_s)
+        for m in range(2):
+            h = keep.tile([P, HALF], F32, name="hb_%d" % m)
+            nc.vector.tensor_scalar(h[:], second[m][:], 0.0625, None, MULT)
+            send(h[:], m, HALF, HALF)
 
         k1b_s, k2b_s = plane_k[:, 0:PAIR], plane_k[:, PAIR:]
         k2b_w = gather_words(d_w, k2_l, PAIR, PAIR, "k2_w")
@@ -205,7 +212,5 @@ def tile_picked_cmixhisendtwo_none_p_kernel(
             h = keep.tile([P, S], F32, name="h_%d" % m)
             nc.vector.tensor_scalar(h[:], acc[:].rearrange("p c j -> p (c j)"), 0.0625, None, MULT)
             send(h[:], 2 + m, 0, S)
-        for m, tag in enumerate(("k1_w", "k2_w", "larger_2")):
-            finish(m, tag, slice(0, S), nc.sync)
-        finish(3, "larger_3a", slice(0, HALF), nc.sync)
-        finish(3, "larger_3b", slice(HALF, S), nc.scalar)
+        for m, tag in enumerate(("k1_w", "k2_w", "larger_2", "larger_3")):
+            finish(m, tag)

@@ -24,7 +24,6 @@ HALF = S // 2
 QUARTER = S // 4
 PAIR = 2 * P
 AL = 64
-CLEAR_SPLIT = G // 4
 
 
 def entries(list_tile, first, count):
@@ -46,10 +45,7 @@ def tile_picked_cmixhisendtwo_none_p_kernel(
         plane_a = keep.tile([P, 2 * PAIR + S], U8, align_bytes=AL, name="plane_a")
         plane_k = keep.tile([P, 2 * PAIR], U8, align_bytes=AL, name="plane_k")
         plane_x = keep.tile([P, S], U8, align_bytes=AL, name="plane_x")
-        nc.vector.memset(x_sc[:].bitcast(I32), 0)
-        nc.vector.memset(d_sc[:, 0:CLEAR_SPLIT].bitcast(I32), 0)
-        nc.gpsimd.memset(d_sc[:, CLEAR_SPLIT:].bitcast(I32), 0)
-        for t in (w_sc, plane_x, plane_a, plane_k):
+        for t in (x_sc, d_sc, w_sc, plane_x, plane_a, plane_k):
             nc.vector.memset(t[:].bitcast(I32), 0)
 
         def load_list(src, name):

from contextlib import ExitStack

import concourse.mybir as mybir

K, T, S, H, G = 512, 1024, 256, 512, 2048
FLOPS = 3 * 2 * K * H * S

F32 = mybir.dt.float32
BF16 = mybir.dt.bfloat16
I32 = mybir.dt.int32
U32 = mybir.dt.uint32
U16 = mybir.dt.uint16
U8 = mybir.dt.uint8
FP8X4 = mybir.dt.float8_e4m3fn_x4
FP4X4 = mybir.dt.float4_e2m1fn_x4
COPY = mybir.ActivationFunctionType.Copy
MULT = mybir.AluOpType.mult
MAX = mybir.AluOpType.max

P = 128
PACK = 4
LANES = 16
HALF = S // 2
QUARTER = S // 4
PAIR = 2 * P
AL = 64


def entries(list_tile, first, count):
    return list_tile[:, first // LANES : (first + count) // LANES]


def tile_picked_cmixhisendtwo_none_p_kernel(
    tc, x_words, x_scales, w1_words, w1_scales, gs, d_words, d_scales, offs, k1, k2, hz, n1, n2, out
):
    nc = tc.nc
    with ExitStack() as ctx:
        lists = ctx.enter_context(tc.tile_pool(name="lists", bufs=1))
        keep = ctx.enter_context(tc.tile_pool(name="keep", bufs=1))
        psum = ctx.enter_context(tc.psum_pool(name="psum", bufs=1))

        d_sc = keep.tile([P, G], U8, align_bytes=AL, name="d_sc")
        x_sc = keep.tile([P, T], U8, align_bytes=AL, name="x_sc")
        w_sc = keep.tile([P, H], U8, align_bytes=AL, name="w_sc")
        plane_a = keep.tile([P, 2 * PAIR + S], U8, align_bytes=AL, name="plane_a")
        plane_k = keep.tile([P, 2 * PAIR], U8, align_bytes=AL, name="plane_k")
        plane_x = keep.tile([P, S], U8, align_bytes=AL, name="plane_x")
        for t in (x_sc, d_sc, w_sc, plane_x, plane_a, plane_k):
            nc.vector.memset(t[:].bitcast(I32), 0)

        def load_list(src, name):
            t = lists.tile(list(src.shape), U16, name=name)
            nc.sync.dma_start(t[:], src)
            return t

        x_w = keep.tile([P, T], U32, align_bytes=AL, name="x_w")
        d_w = keep.tile([P, G], U32, align_bytes=AL, name="d_w")
        w_w = keep.tile([P, 2 * H], U8, align_bytes=AL, name="w_w")
        nc.scalar.dma_start(w_w[:].bitcast(I32), w1_words[0].bitcast(I32))
        nc.scalar.dma_start(x_sc[0:P:8, :].bitcast(I32), x_scales[0].bitcast(I32))
        nc.scalar.dma_start(d_sc[0:P:8, :].bitcast(I32), d_scales[0].bitcast(I32))
        nc.scalar.dma_start(x_w[:].bitcast(I32), x_words[0].rearrange("p n t -> p (n t)").bitcast(I32))

        offs_l = load_list(offs, "offs_l")
        k1_l = load_list(k1, "k1_l")
        hz_l = load_list(hz, "hz_l")
        k2_l = load_list(k2, "k2_l")
        for q in range(4):
            queue = nc.sync if q < 3 else nc.scalar
            queue.dma_start(w_sc[32 * q : 32 * q + 4, :].bitcast(I32), w1_scales[0, 4 * q : 4 * q + 4, :].bitcast(I32))
        nc.sync.dma_start(d_w[:].bitcast(I32), d_words[0].rearrange("p n t -> p (n t)").bitcast(I32))
        gain = keep.tile([P, PACK], F32, name="gain")
        nc.gpsimd.dma_start(gain[:], gs.rearrange("(p t) o -> p (t o)", t=PACK))

        w_dw = keep.tile([P, 2 * H], U8, align_bytes=AL, name="w_dw")
        w_ds = keep.tile([P, H], U8, align_bytes=AL, name="w_ds")
        nc.scalar.copy(
            w_dw[:].bitcast(U16).rearrange("p (t m) -> p t m", t=PACK),
            w_w[:].bitcast(U16).rearrange("p (m t) -> p t m", t=PACK),
        )
        nc.gpsimd.tensor_copy(
            w_ds[:].rearrange("p (t m) -> p t m", t=PACK),
            w_sc[:].rearrange("p (m t) -> p t m", t=PACK),
        )

        def gather(dst, window, offsets):
            nc.vector.tensor_copy(dst, window[:].indirect(offsets))

        def gather_bytes(jobs, picked):
            at = 0
            for window, list_tile, first, n in jobs:
                gather(picked[:, at : at + n], window, entries(list_tile, first, n))
                at = at + n

        def place_rows(plane, picked, rows, queues):
            for r in rows:
                queues[r % len(queues)].dma_start(plane[r:P:32, :].bitcast(I32), picked[8 * r : P : 32, :].bitcast(I32))

        def gather_words(window, list_tile, first, n, tag):
            words = keep.tile([P, n], U32, align_bytes=AL, tag=tag, name="words")
            gather(words[:], window, entries(list_tile, first, n))
            return words

        def project(xo_w, xo_s, z, tag, bank):
            y = psum.tile([P, PACK, HALF], F32, tag=bank, name="y")
            for t in range(PACK):
                nc.tensor.matmul_mx(
                    y[:, t, :],
                    lhsT=w_dw[:, 2 * P * t : 2 * P * (t + 1)].bitcast(FP4X4),
                    lhsT_scale=w_ds[:, P * t : P * (t + 1)],
                    rhs=xo_w[:].bitcast(FP8X4),
                    rhs_scale=xo_s,
                    start=True,
                    stop=True,
                )
            z_w = keep.tile([P, HALF], U32, align_bytes=AL, tag="zw_" + tag, name="z_w")
            z_s = keep.tile([P, HALF], U8, align_bytes=AL, tag="zs_" + tag, name="z_s")
            parts = [slice(0, QUARTER), slice(QUARTER, HALF)]
            for c in range(2):
                nc.vector.tensor_tensor(
                    z[:, parts[c], :], y[:, :, parts[c]].rearrange("p t j -> p j t"),
                    gain[:].unsqueeze(1).to_broadcast([P, QUARTER, PACK]), MULT,
                )
            for c in range(2):
                nc.vector.quantize_mx(z_w[:, parts[c]].bitcast(FP8X4), z_s[:, parts[c]], z[:, parts[c], :].rearrange("p j t -> p (j t)"))
            return z_w, z_s

        def hashed_pass(acc, k2_w, k2_s, m, hz_w, hz_s):
            nc.tensor.matmul_mx(
                acc, lhsT=k2_w[:, P * m : P * (m + 1)].bitcast(FP8X4), lhsT_scale=k2_s[:, P * m : P * (m + 1)],
                rhs=hz_w[:].bitcast(FP8X4), rhs_scale=hz_s, start=True, stop=False,
            )

        def projected_pass(acc, k1_w, k1_s, m, z_w, z_s):
            nc.tensor.matmul_mx(
                acc, lhsT=k1_w[:, P * m : P * (m + 1)].bitcast(FP8X4), lhsT_scale=k1_s[:, P * m : P * (m + 1)],
                rhs=z_w[:].bitcast(FP8X4), rhs_scale=z_s[:], start=False, stop=True,
            )

        widths = [S, S, 2 * S, 2 * S]
        ds1 = [keep.tile([P, widths[m]], F32, name="ds1_%d" % m) for m in range(4)]
        ds2 = [keep.tile([P, widths[m]], F32, name="ds2_%d" % m) for m in range(4)]

        def send(h, m, first, n):
            nc.scalar.activation(ds1[m][:].indirect(entries(n1_l, first, n)), h, COPY)
            nc.scalar.activation(ds2[m][:].indirect(entries(n2_l, first, n)), h, COPY)

        def finish(m, tag):
            larger = keep.tile([P, S], F32, align_bytes=AL, tag=tag, name="larger")
            nc.vector.tensor_tensor(larger[:], ds1[m][:, 0:S], ds2[m][:, 0:S], MAX)
            nc.sync.dma_start(out[P * m : P * (m + 1), :], larger[:])

        picked_x = keep.tile([P, S], U8, align_bytes=AL, name="picked_x")
        gather_bytes([(x_sc, offs_l, 0, S)], picked_x)
        place_rows(plane_x, picked_x, range(4), [nc.sync])
        xoa_s, xob_s = plane_x[:, 0:HALF], plane_x[:, HALF:]
        picked_a = keep.tile([P, 2 * PAIR + S], U8, align_bytes=AL, name="picked_a")
        gather_bytes([(d_sc, k1_l, 0, PAIR), (d_sc, k2_l, 0, PAIR), (x_sc, hz_l, 0, S)], picked_a)
        place_rows(plane_a, picked_a, range(4), [nc.sync])
        k1a_s, k2a_s = plane_a[:, 0:PAIR], plane_a[:, PAIR : 2 * PAIR]
        hza_s, hzb_s = plane_a[:, 2 * PAIR : 2 * PAIR + HALF], plane_a[:, 2 * PAIR + HALF :]
        n1_l = load_list(n1, "n1_l")
        n2_l = load_list(n2, "n2_l")
        xoa_w = gather_words(x_w, offs_l, 0, HALF, "xo_w")
        hza_w = gather_words(x_w, hz_l, 0, HALF, "hza_w")
        hzb_w = gather_words(x_w, hz_l, HALF, HALF, "hzb_w")
        xob_w = gather_words(x_w, offs_l, HALF, HALF, "xob_w")
        k2a_w = gather_words(d_w, k2_l, 0, PAIR, "k2_w")
        k1a_w = gather_words(d_w, k1_l, 0, PAIR, "k1_w")
        z_a = keep.tile([P, HALF, PACK], BF16, align_bytes=AL, tag="z_a", name="z_a")
        za_w, za_s = project(xoa_w, xoa_s, z_a, "a", "y_a")
        first = [psum.tile([P, HALF], F32, tag="first_%d" % m, name="first") for m in range(2)]
        for m in range(2):
            hashed_pass(first[m][:], k2a_w, k2a_s, m, hza_w, hza_s)
        for m in range(2):
            projected_pass(first[m][:], k1a_w, k1a_s, m, za_w, za_s)
        h0 = keep.tile([P, HALF], F32, align_bytes=AL, tag="h0", name="h0")
        nc.scalar.activation(h0[:], first[0][:], COPY, scale=0.0625)
        send(h0[:], 0, 0, HALF)
        h1 = keep.tile([P, HALF], F32, align_bytes=AL, tag="h1", name="h1")
        nc.vector.tensor_scalar(h1[:], first[1][:], 0.0625, None, MULT)
        send(h1[:], 1, 0, HALF)

        picked_k = keep.tile([P, 2 * PAIR], U8, align_bytes=AL, tag="z_a", name="picked_k")
        gather_bytes([(d_sc, k1_l, PAIR, PAIR), (d_sc, k2_l, PAIR, PAIR)], picked_k)
        place_rows(plane_k, picked_k, range(4), [nc.sync])
        z_b = keep.tile([P, HALF, PACK], BF16, align_bytes=AL, name="z_b")
        zb_w, zb_s = project(xob_w, xob_s, z_b, "b", "first_0")
        second = [psum.tile([P, HALF], F32, name="second_%d" % m) for m in range(2)]
        for m in range(2):
            hashed_pass(second[m][:], k2a_w, k2a_s, m, hzb_w, hzb_s)
        for m in range(2):
            projected_pass(second[m][:], k1a_w, k1a_s, m, zb_w, zb_s)
        for m in range(2):
            h = keep.tile([P, HALF], F32, name="hb_%d" % m)
            nc.vector.tensor_scalar(h[:], second[m][:], 0.0625, None, MULT)
            send(h[:], m, HALF, HALF)

        k1b_s, k2b_s = plane_k[:, 0:PAIR], plane_k[:, PAIR:]
        k2b_w = gather_words(d_w, k2_l, PAIR, PAIR, "k2_w")
        k1b_w = gather_words(d_w, k1_l, PAIR, PAIR, "k1_w")
        halves = [(hza_w, hza_s, za_w, za_s), (hzb_w, hzb_s, zb_w, zb_s)]
        for m in range(2):
            acc = psum.tile([P, 2, HALF], F32, name="acc_%d" % m)
            for c, (hz_w, hz_s, z_w, z_s) in enumerate(halves):
                hashed_pass(acc[:, c, :], k2b_w, k2b_s, m, hz_w, hz_s)
                projected_pass(acc[:, c, :], k1b_w, k1b_s, m, z_w, z_s)
            h = keep.tile([P, S], F32, name="h_%d" % m)
            nc.vector.tensor_scalar(h[:], acc[:].rearrange("p c j -> p (c j)"), 0.0625, None, MULT)
            send(h[:], 2 + m, 0, S)
        for m, tag in enumerate(("k1_w", "k2_w", "larger_2", "larger_3")):
            finish(m, tag)
